import numpy as np
import ml_dtypes


def mxq(x, axis, fmt="e4m3"):
    dtype, down = {"e4m3": (ml_dtypes.float8_e4m3fn, 7), "e5m2": (ml_dtypes.float8_e5m2, 14)}[fmt]
    v = np.moveaxis(np.asarray(x, np.float32).astype(ml_dtypes.bfloat16).astype(np.float64), axis, -1)
    blocks = v.reshape(v.shape[:-1] + (-1, 32))
    amax = np.abs(blocks).max(-1, keepdims=True)
    byte = np.maximum(np.where(amax > 0, np.frexp(amax)[1] - 1 + 127, 0) - down, 1)
    scale = np.exp2(byte - 127.0)
    codes = (blocks / scale).astype(np.float32).astype(dtype).astype(np.float64)
    return np.moveaxis((codes * scale).reshape(v.shape), -1, axis)


WIDE = False


def mx_kscale(k):
    if not WIDE:
        return np.ones(k)
    levels = np.array([10, -10, 5, -5, 0])
    if k % 512:
        return np.exp2(np.random.permutation(np.resize(levels, k // 32))).repeat(32)
    a = np.empty((k // 512, 16))
    for p in range(k // 512):
        a[p, :8] = np.random.permutation(np.resize(levels, 8))
        for g in range(8):
            far = levels[np.abs(levels - a[p, g]) >= 10]
            a[p, g + 8] = far[np.random.randint(len(far))]
    return np.exp2(a.ravel()).repeat(32)


def f64(x):
    return np.asarray(x).astype(np.float64)


def striped(idx):
    return np.tile(idx.reshape(-1, 16).T, (8, 1)).astype(np.uint16)


def unstriped(offs):
    return offs[:16].T.reshape(-1).astype(np.int64)


def silu(v):
    return v / (1.0 + np.exp(-np.maximum(v, -700.0)))


K, T, D, S, V, N = 1024, 2048, 3, 512, 256, 512


def setup_inputs():
    n = np.random.standard_normal
    s = mx_kscale(K)[:, None]
    return {
        "xT": (n((K, T)) * s).astype(np.float32),
        "w": (n((K, N)) / np.sqrt(K) / s).astype(np.float32),
        "b": (0.3 * n((N, 1))).astype(np.float32),
        "gate": np.tile(np.random.uniform(0.2, 1.0, (D, 1, V)) / np.sqrt(D), (1, N, 1)).astype(np.float32),
        "offs": striped(np.random.permutation(T)[:S]),
        "pos1": striped(np.random.permutation(S)[:V]),
        "pos2": striped(np.random.permutation(S)[:V]),
        "pos3": striped(np.random.permutation(S)[:V]),
    }


def reference(xT, w, b, gate, offs, pos1, pos2, pos3):
    idx = unstriped(offs)
    xq = mxq(f64(xT)[:, idx], 0, "e4m3")
    y = mxq(f64(w), 0, "e4m3").T @ xq
    y = silu(y + f64(b))
    return sum(f64(gate[d]) * y[:, unstriped(p)] for d, p in enumerate((pos1, pos2, pos3)))

@@ -1,0 +1,199 @@
+from contextlib import ExitStack
+
+import concourse.mybir as mybir
+
+K, T, D, S, V, N = 1024, 2048, 3, 512, 256, 512
+FLOPS = 2 * K * S * N
+
+F32 = mybir.dt.float32
+BF16 = mybir.dt.bfloat16
+U32 = mybir.dt.uint32
+U16 = mybir.dt.uint16
+U8 = mybir.dt.uint8
+FP8X4 = mybir.dt.float8_e4m3fn_x4
+MULT = mybir.AluOpType.mult
+ADD = mybir.AluOpType.add
+SILU = mybir.ActivationFunctionType.Silu
+
+P = 128
+PACK = 4
+K_PASS = P * PACK
+PASSES = K // K_PASS
+BLOCKS = N // P
+HALF = S // 2
+
+
+def tile_picked_sub_lin_silu_sub_e_kernel(tc, xT, w, b, gate, offs, pos1, pos2, pos3, out):
+    nc = tc.nc
+    with ExitStack() as ctx:
+        lists = ctx.enter_context(tc.tile_pool(name="lists", bufs=1))
+        keep = ctx.enter_context(tc.tile_pool(name="keep", bufs=1))
+        psum = ctx.enter_context(tc.psum_pool(name="psum", bufs=1))
+
+        offs_sb = lists.tile([P, S // 16], U16, name="offs_sb")
+        nc.sync.dma_start(offs_sb[:], offs)
+
+        b_rows = keep.tile([P, 32], F32, name="b_rows", align_bytes=64)
+        nc.vector.memset(b_rows[:], 0.0)
+        for c in range(BLOCKS):
+            nc.scalar.dma_start(
+                b_rows[c:P:32, :], b[c * P : (c + 1) * P, :].rearrange("(q i) o -> q (i o)", i=32)
+            )
+        bias = keep.tile([P, 32], F32, name="bias", align_bytes=64)
+        nc.vector.transpose(bias[:], b_rows[:])
+
+        warm = keep.tile([P, 8], F32, name="warm")
+        nc.gpsimd.memset(warm[:], 0.0)
+        warmed = keep.tile([P, 8], F32, name="warmed")
+        nc.scalar.activation(warmed[:], warm[:], SILU)
+
+        planes = {}
+        for a in range(PASSES):
+            rows = xT[a * K_PASS : (a + 1) * K_PASS, :].rearrange("(p j) t -> p j t", j=PACK)
+            for j in range(PACK):
+                plane = keep.tile([P, T], F32, name=f"x{a}{j}")
+                nc.sync.dma_start(plane[:], rows[:, j, :])
+                planes[a, j] = plane
+
+        def load_w(a, c, blocks):
+            raw = keep.tile([P, PACK, blocks * P], F32, name=f"wraw{a}{c}")
+            rows = w[a * K_PASS : (a + 1) * K_PASS, c * P : (c + blocks) * P]
+            nc.sync.dma_start(raw[:], rows.rearrange("(p j) m -> p j m", j=PACK))
+            return raw
+
+        def load_gate(c):
+            g = keep.tile([P, D, V], F32, name=f"gate{c}")
+            nc.sync.dma_start(g[:], gate[:, c * P : (c + 1) * P, :].rearrange("d m v -> m d v"))
+            return g
+
+        raw0 = [load_w(a, 0, 1) for a in range(PASSES)]
+        raw1 = [load_w(a, 1, 1) for a in range(PASSES)]
+        pos_sb = []
+        for d, pos in enumerate((pos1, pos2, pos3)):
+            pos_tile = lists.tile([P, V // 16], U16, name=f"pos_sb{d}")
+            nc.sync.dma_start(pos_tile[:], pos)
+            pos_sb.append(pos_tile)
+        gates = [load_gate(0)]
+        raw2 = [load_w(a, 2, 2) for a in range(PASSES)]
+        for c in range(1, BLOCKS):
+            gates.append(load_gate(c))
+
+        xb, xq, xs = [], [], []
+        for a in range(PASSES):
+            xb.append(keep.tile([P, S, PACK], BF16, name=f"xb{a}", align_bytes=64))
+            xq.append(keep.tile([P, S], U32, name=f"xq{a}", align_bytes=64))
+            xs.append(keep.tile([P, S], U8, name=f"xs{a}", align_bytes=64))
+
+        def gather(a, j, lo, hi):
+            nc.vector.tensor_copy(
+                xb[a][:, lo:hi, j], planes[a, j][:].indirect(offs_sb[:, lo // 16 : hi // 16])
+            )
+
+        def quantise_x(a, lo, hi):
+            nc.vector.quantize_mx(
+                out=xq[a][:, lo:hi].bitcast(FP8X4),
+                scales=xs[a][:, lo:hi],
+                in_=xb[a][:, lo:hi, :].rearrange("p s j -> p (s j)"),
+            )
+
+        for j in range(PACK):
+            gather(0, j, 0, S)
+        gather(1, 0, 0, S)
+        quantise_x(0, 0, S)
+        gather(1, 1, 0, S)
+        gather(1, 2, 0, S)
+        gather(1, 3, 0, HALF)
+        gather(1, 3, HALF, S)
+        quantise_x(1, 0, HALF)
+
+        def interleave_w(wb, raw):
+            nc.scalar.copy(wb, raw[:].rearrange("p j m -> p m j"))
+
+        def quantise_w(wq, ws, wb):
+            nc.vector.quantize_mx(out=wq.bitcast(FP8X4), scales=ws, in_=wb)
+
+        wq0 = keep.tile([P, PASSES, P], U32, name="wq0", align_bytes=64)
+        ws0 = keep.tile([P, PASSES, P], U8, name="ws0", align_bytes=64)
+        wb0 = keep.tile([P, PASSES, P, PACK], BF16, name="wb0", align_bytes=64)
+        for a in range(PASSES):
+            interleave_w(wb0[:, a], raw0[a])
+        quantise_w(wq0[:, 0], ws0[:, 0], wb0[:, 0].rearrange("p m j -> p (m j)"))
+        quantise_x(1, HALF, S)
+        quantise_w(wq0[:, 1], ws0[:, 1], wb0[:, 1].rearrange("p m j -> p (m j)"))
+
+        def prepare_w(c, raws, blocks):
+            m = blocks * P
+            wq = keep.tile([P, PASSES, m], U32, name=f"wq{c}", align_bytes=64)
+            ws = keep.tile([P, PASSES, m], U8, name=f"ws{c}", align_bytes=64)
+            wb = keep.tile([P, PASSES, m, PACK], BF16, name=f"wb{c}", align_bytes=64)
+            for a in range(PASSES):
+                interleave_w(wb[:, a], raws[a])
+            quantise_w(
+                wq[:].rearrange("p a m -> p (a m)"),
+                ws[:].rearrange("p a m -> p (a m)"),
+                wb[:].rearrange("p a m j -> p (a m j)"),
+            )
+            return wq, ws
+
+        def product(acc, wq, ws, cols, lo, hi):
+            for a in range(PASSES):
+                nc.tensor.matmul_mx(
+                    out=acc,
+                    lhsT=wq[:, a, cols].bitcast(FP8X4),
+                    lhsT_scale=ws[:, a, cols],
+                    rhs=xq[a][:, lo:hi].bitcast(FP8X4),
+                    rhs_scale=xs[a][:, lo:hi],
+                    start=(a == 0),
+                    stop=(a == PASSES - 1),
+                )
+
+        def results(c, wq, ws, cols, step):
+            y = keep.tile([P, S], F32, name=f"y{c}")
+            for lo in range(0, S, step):
+                acc = psum.tile([P, step], F32, name=f"acc{c}{lo}")
+                product(acc[:], wq, ws, cols, lo, lo + step)
+                nc.scalar.activation(y[:, lo : lo + step], acc[:], SILU, bias=bias[:, c : c + 1])
+            return y
+
+        ys = [results(0, wq0, ws0, slice(0, P), HALF)]
+        wq1, ws1 = prepare_w(1, raw1, 1)
+        ys.append(results(1, wq1, ws1, slice(0, P), S))
+        wq2, ws2 = prepare_w(2, raw2, 2)
+        ys.append(results(2, wq2, ws2, slice(0, P), S))
+        ys.append(results(3, wq2, ws2, slice(P, 2 * P), S))
+
+        terms = [keep.tile([P, D, V], F32, name=f"terms{c}") for c in range(BLOCKS)]
+        sums = [keep.tile([P, V], F32, name=f"sums{c}") for c in range(BLOCKS)]
+        outs = [keep.tile([P, V], F32, name=f"outs{c}") for c in range(BLOCKS)]
+
+        def fetch(c, d, lo, hi):
+            nc.vector.tensor_tensor(
+                terms[c][:, d, lo:hi],
+                ys[c][:].indirect(pos_sb[d][:, lo // 16 : hi // 16]),
+                gates[c][:, d, lo:hi],
+                MULT,
+            )
+
+        def add_first(c):
+            nc.vector.tensor_tensor(sums[c][:], terms[c][:, 0, :], terms[c][:, 1, :], ADD)
+
+        def add_last(c, lo, hi):
+            nc.vector.tensor_tensor(outs[c][:, lo:hi], sums[c][:, lo:hi], terms[c][:, 2, lo:hi], ADD)
+            nc.sync.dma_start(out[c * P : (c + 1) * P, lo:hi], outs[c][:, lo:hi])
+
+        for c in range(BLOCKS):
+            last = c == BLOCKS - 1
+            fetch(c, 0, 0, V)
+            if c > 0:
+                add_first(c - 1)
+            fetch(c, 1, 0, V)
+            if c > 0:
+                add_last(c - 1, 0, V)
+            if last:
+                fetch(c, 2, 0, V // 2)
+                add_first(c)
+                fetch(c, 2, V // 2, V)
+                add_last(c, 0, V // 2)
+                add_last(c, V // 2, V)
+            else:
+                fetch(c, 2, 0, V)

@@ -20,7 +20,7 @@ PACK = 4
 K_PASS = P * PACK
 PASSES = K // K_PASS
 BLOCKS = N // P
-HALF = S // 2
+PIECES = [(0, 256), (256, 512)]
 
 
 def tile_picked_sub_lin_silu_sub_e_kernel(tc, xT, w, b, gate, offs, pos1, pos2, pos3, out):
@@ -35,58 +35,72 @@ def tile_picked_sub_lin_silu_sub_e_kernel(tc, xT, w, b, gate, offs, pos1, pos2, 
 
         b_rows = keep.tile([P, 32], F32, name="b_rows", align_bytes=64)
         nc.vector.memset(b_rows[:], 0.0)
-        for c in range(BLOCKS):
-            nc.scalar.dma_start(
-                b_rows[c:P:32, :], b[c * P : (c + 1) * P, :].rearrange("(q i) o -> q (i o)", i=32)
-            )
-        bias = keep.tile([P, 32], F32, name="bias", align_bytes=64)
-        nc.vector.transpose(bias[:], b_rows[:])
-
         warm = keep.tile([P, 8], F32, name="warm")
         nc.gpsimd.memset(warm[:], 0.0)
         warmed = keep.tile([P, 8], F32, name="warmed")
         nc.scalar.activation(warmed[:], warm[:], SILU)
 
+        def load_bias():
+            for c in range(BLOCKS):
+                nc.sync.dma_start(
+                    b_rows[c:P:32, :], b[c * P : (c + 1) * P, :].rearrange("(q i) o -> q (i o)", i=32)
+                )
+
         planes = {}
-        for a in range(PASSES):
+        for a, j0, count in ((0, 0, 1), (0, 1, 1), (0, 2, 1), (0, 3, 1), (1, 0, 1), (1, 1, 1), (1, 2, 1), (1, 3, 1)):
+            if (a, j0) == (1, 0):
+                load_bias()
             rows = xT[a * K_PASS : (a + 1) * K_PASS, :].rearrange("(p j) t -> p j t", j=PACK)
-            for j in range(PACK):
-                plane = keep.tile([P, T], F32, name=f"x{a}{j}")
-                nc.sync.dma_start(plane[:], rows[:, j, :])
-                planes[a, j] = plane
+            group = keep.tile([P, count, T], F32, name=f"x{a}{j0}")
+            nc.sync.dma_start(group[:], rows[:, j0 : j0 + count, :])
+            for j in range(count):
+                planes[a, j0 + j] = group[:, j, :]
+
+        raws = {}
 
         def load_w(a, c, blocks):
             raw = keep.tile([P, PACK, blocks * P], F32, name=f"wraw{a}{c}")
             rows = w[a * K_PASS : (a + 1) * K_PASS, c * P : (c + blocks) * P]
             nc.sync.dma_start(raw[:], rows.rearrange("(p j) m -> p j m", j=PACK))
-            return raw
+            raws[a, c] = raw
+
+        gates = []
 
         def load_gate(c):
             g = keep.tile([P, D, V], F32, name=f"gate{c}")
             nc.sync.dma_start(g[:], gate[:, c * P : (c + 1) * P, :].rearrange("d m v -> m d v"))
-            return g
+            gates.append(g)
 
-        raw0 = [load_w(a, 0, 1) for a in range(PASSES)]
-        raw1 = [load_w(a, 1, 1) for a in range(PASSES)]
+        for c in (0, 1):
+            for a in range(PASSES):
+                load_w(a, c, 1)
         pos_sb = []
         for d, pos in enumerate((pos1, pos2, pos3)):
             pos_tile = lists.tile([P, V // 16], U16, name=f"pos_sb{d}")
             nc.sync.dma_start(pos_tile[:], pos)
             pos_sb.append(pos_tile)
-        gates = [load_gate(0)]
-        raw2 = [load_w(a, 2, 2) for a in range(PASSES)]
+        load_gate(0)
+        for a in range(PASSES):
+            load_w(a, 2, 2)
         for c in range(1, BLOCKS):
-            gates.append(load_gate(c))
+            load_gate(c)
 
         xb, xq, xs = [], [], []
         for a in range(PASSES):
             xb.append(keep.tile([P, S, PACK], BF16, name=f"xb{a}", align_bytes=64))
             xq.append(keep.tile([P, S], U32, name=f"xq{a}", align_bytes=64))
             xs.append(keep.tile([P, S], U8, name=f"xs{a}", align_bytes=64))
+        picked = [keep.tile([P, PACK, S], F32, name=f"picked{a}") for a in range(PASSES)]
+
+        def gather_wide(a, j):
+            nc.vector.tensor_copy(picked[a][:, j, :], planes[a, j].indirect(offs_sb[:]))
 
         def gather(a, j, lo, hi):
-            nc.vector.tensor_copy(
-                xb[a][:, lo:hi, j], planes[a, j][:].indirect(offs_sb[:, lo // 16 : hi // 16])
+            nc.vector.tensor_copy(xb[a][:, lo:hi, j], planes[a, j].indirect(offs_sb[:, lo // 16 : hi // 16]))
+
+        def interleave_x(a, j0, j1, lo, hi):
+            nc.scalar.copy(
+                xb[a][:, lo:hi, j0:j1], picked[a][:, j0:j1, lo:hi].rearrange("p j s -> p s j")
             )
 
         def quantise_x(a, lo, hi):
@@ -97,70 +111,71 @@ def tile_picked_sub_lin_silu_sub_e_kernel(tc, xT, w, b, gate, offs, pos1, pos2, 
             )
 
         for j in range(PACK):
-            gather(0, j, 0, S)
-        gather(1, 0, 0, S)
+            gather_wide(0, j)
+        for lo in (0, S // 2):
+            interleave_x(0, 0, PACK, lo, lo + S // 2)
+        gather_wide(1, 0)
+        gather_wide(1, 1)
+        interleave_x(1, 0, 2, 0, S)
         quantise_x(0, 0, S)
-        gather(1, 1, 0, S)
         gather(1, 2, 0, S)
-        gather(1, 3, 0, HALF)
-        gather(1, 3, HALF, S)
-        quantise_x(1, 0, HALF)
+        gather(1, 3, 0, S // 2)
+        gather(1, 3, S // 2, S)
+        for lo, hi in PIECES:
+            quantise_x(1, lo, hi)
 
-        def interleave_w(wb, raw):
-            nc.scalar.copy(wb, raw[:].rearrange("p j m -> p m j"))
+        bias = keep.tile([P, 32], F32, name="bias", align_bytes=64)
+        nc.vector.transpose(bias[:], b_rows[:])
 
-        def quantise_w(wq, ws, wb):
-            nc.vector.quantize_mx(out=wq.bitcast(FP8X4), scales=ws, in_=wb)
+        weights = {}
 
-        wq0 = keep.tile([P, PASSES, P], U32, name="wq0", align_bytes=64)
-        ws0 = keep.tile([P, PASSES, P], U8, name="ws0", align_bytes=64)
-        wb0 = keep.tile([P, PASSES, P, PACK], BF16, name="wb0", align_bytes=64)
-        for a in range(PASSES):
-            interleave_w(wb0[:, a], raw0[a])
-        quantise_w(wq0[:, 0], ws0[:, 0], wb0[:, 0].rearrange("p m j -> p (m j)"))
-        quantise_x(1, HALF, S)
-        quantise_w(wq0[:, 1], ws0[:, 1], wb0[:, 1].rearrange("p m j -> p (m j)"))
-
-        def prepare_w(c, raws, blocks):
+        def prepare_w(c, blocks, joined):
             m = blocks * P
             wq = keep.tile([P, PASSES, m], U32, name=f"wq{c}", align_bytes=64)
             ws = keep.tile([P, PASSES, m], U8, name=f"ws{c}", align_bytes=64)
             wb = keep.tile([P, PASSES, m, PACK], BF16, name=f"wb{c}", align_bytes=64)
             for a in range(PASSES):
-                interleave_w(wb[:, a], raws[a])
-            quantise_w(
-                wq[:].rearrange("p a m -> p (a m)"),
-                ws[:].rearrange("p a m -> p (a m)"),
-                wb[:].rearrange("p a m j -> p (a m j)"),
-            )
-            return wq, ws
-
-        def product(acc, wq, ws, cols, lo, hi):
-            for a in range(PASSES):
-                nc.tensor.matmul_mx(
-                    out=acc,
-                    lhsT=wq[:, a, cols].bitcast(FP8X4),
-                    lhsT_scale=ws[:, a, cols],
-                    rhs=xq[a][:, lo:hi].bitcast(FP8X4),
-                    rhs_scale=xs[a][:, lo:hi],
-                    start=(a == 0),
-                    stop=(a == PASSES - 1),
+                nc.scalar.copy(
+                    wb[:, a].rearrange("p (g i) j -> p g j i", i=4),
+                    raws[a, c][:].rearrange("p j (g i) -> p g j i", i=4),
                 )
+                if not joined:
+                    nc.vector.quantize_mx(
+                        out=wq[:, a].bitcast(FP8X4), scales=ws[:, a], in_=wb[:, a].rearrange("p m j -> p (m j)")
+                    )
+            if joined:
+                nc.vector.quantize_mx(
+                    out=wq[:].rearrange("p a m -> p (a m)").bitcast(FP8X4),
+                    scales=ws[:].rearrange("p a m -> p (a m)"),
+                    in_=wb[:].rearrange("p a m j -> p (a m j)"),
+                )
+            for i in range(blocks):
+                for a in range(PASSES):
+                    weights[c + i, a] = (wq[:, a, i * P : (i + 1) * P], ws[:, a, i * P : (i + 1) * P])
 
-        def results(c, wq, ws, cols, step):
+        def results(c, pieces):
             y = keep.tile([P, S], F32, name=f"y{c}")
-            for lo in range(0, S, step):
-                acc = psum.tile([P, step], F32, name=f"acc{c}{lo}")
-                product(acc[:], wq, ws, cols, lo, lo + step)
-                nc.scalar.activation(y[:, lo : lo + step], acc[:], SILU, bias=bias[:, c : c + 1])
-            return y
+            for lo, hi in pieces:
+                acc = psum.tile([P, hi - lo], F32, name=f"acc{c}{lo}")
+                for a in range(PASSES):
+                    wq, ws = weights[c, a]
+                    nc.tensor.matmul_mx(
+                        out=acc[:],
+                        lhsT=wq.bitcast(FP8X4),
+                        lhsT_scale=ws,
+                        rhs=xq[a][:, lo:hi].bitcast(FP8X4),
+                        rhs_scale=xs[a][:, lo:hi],
+                        start=(a == 0),
+                        stop=(a == PASSES - 1),
+                    )
+                nc.scalar.activation(y[:, lo:hi], acc[:], SILU, bias=bias[:, c : c + 1])
+            ys.append(y)
 
-        ys = [results(0, wq0, ws0, slice(0, P), HALF)]
-        wq1, ws1 = prepare_w(1, raw1, 1)
-        ys.append(results(1, wq1, ws1, slice(0, P), S))
-        wq2, ws2 = prepare_w(2, raw2, 2)
-        ys.append(results(2, wq2, ws2, slice(0, P), S))
-        ys.append(results(3, wq2, ws2, slice(P, 2 * P), S))
+        ys = []
+        prepare_w(0, 1, False)
+        results(0, PIECES)
+        prepare_w(1, 1, True)
+        results(1, [(0, S)])
 
         terms = [keep.tile([P, D, V], F32, name=f"terms{c}") for c in range(BLOCKS)]
         sums = [keep.tile([P, V], F32, name=f"sums{c}") for c in range(BLOCKS)]
@@ -185,10 +200,12 @@ def tile_picked_sub_lin_silu_sub_e_kernel(tc, xT, w, b, gate, offs, pos1, pos2, 
             last = c == BLOCKS - 1
             fetch(c, 0, 0, V)
             if c > 0:
-                add_first(c - 1)
-            fetch(c, 1, 0, V)
-            if c > 0:
                 add_last(c - 1, 0, V)
+            fetch(c, 1, 0, V)
+            if c == 0:
+                prepare_w(2, 2, True)
+                results(2, [(0, S)])
+                results(3, [(0, S)])
             if last:
                 fetch(c, 2, 0, V // 2)
                 add_first(c)
@@ -197,3 +214,4 @@ def tile_picked_sub_lin_silu_sub_e_kernel(tc, xT, w, b, gate, offs, pos1, pos2, 
                 add_last(c, V // 2, V)
             else:
                 fetch(c, 2, 0, V)
+                add_first(c)

@@ -20,7 +20,7 @@ PACK = 4
 K_PASS = P * PACK
 PASSES = K // K_PASS
 BLOCKS = N // P
-PIECES = [(0, 256), (256, 512)]
+PIECES = [(0, 256), (256, 384), (384, 512)]
 
 
 def tile_picked_sub_lin_silu_sub_e_kernel(tc, xT, w, b, gate, offs, pos1, pos2, pos3, out):
@@ -177,41 +177,42 @@ def tile_picked_sub_lin_silu_sub_e_kernel(tc, xT, w, b, gate, offs, pos1, pos2, 
         prepare_w(1, 1, True)
         results(1, [(0, S)])
 
-        terms = [keep.tile([P, D, V], F32, name=f"terms{c}") for c in range(BLOCKS)]
-        sums = [keep.tile([P, V], F32, name=f"sums{c}") for c in range(BLOCKS)]
-        outs = [keep.tile([P, V], F32, name=f"outs{c}") for c in range(BLOCKS)]
+        terms, sums, outs = {}, {}, {}
+        for c0, count in ((0, 2), (2, 1), (3, 1)):
+            terms[c0] = keep.tile([P, count, D, V], F32, name=f"terms{c0}")
+            sums[c0] = keep.tile([P, count, V], F32, name=f"sums{c0}")
+            outs[c0] = keep.tile([P, count, V], F32, name=f"outs{c0}")
 
-        def fetch(c, d, lo, hi):
+        def fetch(c, d, c0):
             nc.vector.tensor_tensor(
-                terms[c][:, d, lo:hi],
-                ys[c][:].indirect(pos_sb[d][:, lo // 16 : hi // 16]),
-                gates[c][:, d, lo:hi],
-                MULT,
+                terms[c0][:, c - c0, d, :], ys[c][:].indirect(pos_sb[d][:]), gates[c][:, d, :], MULT
             )
 
-        def add_first(c):
-            nc.vector.tensor_tensor(sums[c][:], terms[c][:, 0, :], terms[c][:, 1, :], ADD)
+        def add_first(c0):
+            nc.vector.tensor_tensor(sums[c0][:], terms[c0][:, :, 0, :], terms[c0][:, :, 1, :], ADD)
 
-        def add_last(c, lo, hi):
-            nc.vector.tensor_tensor(outs[c][:, lo:hi], sums[c][:, lo:hi], terms[c][:, 2, lo:hi], ADD)
-            nc.sync.dma_start(out[c * P : (c + 1) * P, lo:hi], outs[c][:, lo:hi])
+        def add_last(c0, count):
+            nc.vector.tensor_tensor(outs[c0][:], sums[c0][:], terms[c0][:, :, 2, :], ADD)
+            rows = out[c0 * P : (c0 + count) * P, :]
+            nc.sync.dma_start(rows.rearrange("(c p) v -> p c v", p=P), outs[c0][:])
 
-        for c in range(BLOCKS):
-            last = c == BLOCKS - 1
-            fetch(c, 0, 0, V)
-            if c > 0:
-                add_last(c - 1, 0, V)
-            fetch(c, 1, 0, V)
-            if c == 0:
-                prepare_w(2, 2, True)
-                results(2, [(0, S)])
-                results(3, [(0, S)])
-            if last:
-                fetch(c, 2, 0, V // 2)
-                add_first(c)
-                fetch(c, 2, V // 2, V)
-                add_last(c, 0, V // 2)
-                add_last(c, V // 2, V)
-            else:
-                fetch(c, 2, 0, V)
-                add_first(c)
+        fetch(0, 0, 0)
+        fetch(0, 1, 0)
+        prepare_w(2, 2, True)
+        results(2, [(0, S)])
+        results(3, [(0, S)])
+        fetch(0, 2, 0)
+        for d in range(D):
+            fetch(1, d, 0)
+        fetch(2, 0, 2)
+        add_first(0)
+        fetch(2, 1, 2)
+        add_last(0, 2)
+        fetch(2, 2, 2)
+        fetch(3, 0, 3)
+        add_first(2)
+        fetch(3, 1, 3)
+        fetch(3, 2, 3)
+        add_first(3)
+        add_last(2, 1)
+        add_last(3, 1)

from contextlib import ExitStack

import concourse.mybir as mybir

K, T, D, S, V, N = 1024, 2048, 3, 512, 256, 512
FLOPS = 2 * K * S * N

F32 = mybir.dt.float32
BF16 = mybir.dt.bfloat16
U32 = mybir.dt.uint32
U16 = mybir.dt.uint16
U8 = mybir.dt.uint8
FP8X4 = mybir.dt.float8_e4m3fn_x4
MULT = mybir.AluOpType.mult
ADD = mybir.AluOpType.add
SILU = mybir.ActivationFunctionType.Silu

P = 128
PACK = 4
K_PASS = P * PACK
PASSES = K // K_PASS
BLOCKS = N // P
PIECES = [(0, 256), (256, 384), (384, 512)]


def tile_picked_sub_lin_silu_sub_e_kernel(tc, xT, w, b, gate, offs, pos1, pos2, pos3, out):
    nc = tc.nc
    with ExitStack() as ctx:
        lists = ctx.enter_context(tc.tile_pool(name="lists", bufs=1))
        keep = ctx.enter_context(tc.tile_pool(name="keep", bufs=1))
        psum = ctx.enter_context(tc.psum_pool(name="psum", bufs=1))

        offs_sb = lists.tile([P, S // 16], U16, name="offs_sb")
        nc.sync.dma_start(offs_sb[:], offs)

        b_rows = keep.tile([P, 32], F32, name="b_rows", align_bytes=64)
        nc.vector.memset(b_rows[:], 0.0)
        warm = keep.tile([P, 8], F32, name="warm")
        nc.gpsimd.memset(warm[:], 0.0)
        warmed = keep.tile([P, 8], F32, name="warmed")
        nc.scalar.activation(warmed[:], warm[:], SILU)

        def load_bias():
            for c in range(BLOCKS):
                nc.sync.dma_start(
                    b_rows[c:P:32, :], b[c * P : (c + 1) * P, :].rearrange("(q i) o -> q (i o)", i=32)
                )

        planes = {}
        for a, j0, count in ((0, 0, 1), (0, 1, 1), (0, 2, 1), (0, 3, 1), (1, 0, 1), (1, 1, 1), (1, 2, 1), (1, 3, 1)):
            if (a, j0) == (1, 0):
                load_bias()
            rows = xT[a * K_PASS : (a + 1) * K_PASS, :].rearrange("(p j) t -> p j t", j=PACK)
            group = keep.tile([P, count, T], F32, name=f"x{a}{j0}")
            nc.sync.dma_start(group[:], rows[:, j0 : j0 + count, :])
            for j in range(count):
                planes[a, j0 + j] = group[:, j, :]

        raws = {}

        def load_w(a, c, blocks):
            raw = keep.tile([P, PACK, blocks * P], F32, name=f"wraw{a}{c}")
            rows = w[a * K_PASS : (a + 1) * K_PASS, c * P : (c + blocks) * P]
            nc.sync.dma_start(raw[:], rows.rearrange("(p j) m -> p j m", j=PACK))
            raws[a, c] = raw

        gates = []

        def load_gate(c):
            g = keep.tile([P, D, V], F32, name=f"gate{c}")
            nc.sync.dma_start(g[:], gate[:, c * P : (c + 1) * P, :].rearrange("d m v -> m d v"))
            gates.append(g)

        for c in (0, 1):
            for a in range(PASSES):
                load_w(a, c, 1)
        pos_sb = []
        for d, pos in enumerate((pos1, pos2, pos3)):
            pos_tile = lists.tile([P, V // 16], U16, name=f"pos_sb{d}")
            nc.sync.dma_start(pos_tile[:], pos)
            pos_sb.append(pos_tile)
        load_gate(0)
        for a in range(PASSES):
            load_w(a, 2, 2)
        for c in range(1, BLOCKS):
            load_gate(c)

        xb, xq, xs = [], [], []
        for a in range(PASSES):
            xb.append(keep.tile([P, S, PACK], BF16, name=f"xb{a}", align_bytes=64))
            xq.append(keep.tile([P, S], U32, name=f"xq{a}", align_bytes=64))
            xs.append(keep.tile([P, S], U8, name=f"xs{a}", align_bytes=64))
        picked = [keep.tile([P, PACK, S], F32, name=f"picked{a}") for a in range(PASSES)]

        def gather_wide(a, j):
            nc.vector.tensor_copy(picked[a][:, j, :], planes[a, j].indirect(offs_sb[:]))

        def gather(a, j, lo, hi):
            nc.vector.tensor_copy(xb[a][:, lo:hi, j], planes[a, j].indirect(offs_sb[:, lo // 16 : hi // 16]))

        def interleave_x(a, j0, j1, lo, hi):
            nc.scalar.copy(
                xb[a][:, lo:hi, j0:j1], picked[a][:, j0:j1, lo:hi].rearrange("p j s -> p s j")
            )

        def quantise_x(a, lo, hi):
            nc.vector.quantize_mx(
                out=xq[a][:, lo:hi].bitcast(FP8X4),
                scales=xs[a][:, lo:hi],
                in_=xb[a][:, lo:hi, :].rearrange("p s j -> p (s j)"),
            )

        for j in range(PACK):
            gather_wide(0, j)
        for lo in (0, S // 2):
            interleave_x(0, 0, PACK, lo, lo + S // 2)
        gather_wide(1, 0)
        gather_wide(1, 1)
        interleave_x(1, 0, 2, 0, S)
        quantise_x(0, 0, S)
        gather(1, 2, 0, S)
        gather(1, 3, 0, S // 2)
        gather(1, 3, S // 2, S)
        for lo, hi in PIECES:
            quantise_x(1, lo, hi)

        bias = keep.tile([P, 32], F32, name="bias", align_bytes=64)
        nc.vector.transpose(bias[:], b_rows[:])

        weights = {}

        def prepare_w(c, blocks, joined):
            m = blocks * P
            wq = keep.tile([P, PASSES, m], U32, name=f"wq{c}", align_bytes=64)
            ws = keep.tile([P, PASSES, m], U8, name=f"ws{c}", align_bytes=64)
            wb = keep.tile([P, PASSES, m, PACK], BF16, name=f"wb{c}", align_bytes=64)
            for a in range(PASSES):
                nc.scalar.copy(
                    wb[:, a].rearrange("p (g i) j -> p g j i", i=4),
                    raws[a, c][:].rearrange("p j (g i) -> p g j i", i=4),
                )
                if not joined:
                    nc.vector.quantize_mx(
                        out=wq[:, a].bitcast(FP8X4), scales=ws[:, a], in_=wb[:, a].rearrange("p m j -> p (m j)")
                    )
            if joined:
                nc.vector.quantize_mx(
                    out=wq[:].rearrange("p a m -> p (a m)").bitcast(FP8X4),
                    scales=ws[:].rearrange("p a m -> p (a m)"),
                    in_=wb[:].rearrange("p a m j -> p (a m j)"),
                )
            for i in range(blocks):
                for a in range(PASSES):
                    weights[c + i, a] = (wq[:, a, i * P : (i + 1) * P], ws[:, a, i * P : (i + 1) * P])

        def results(c, pieces):
            y = keep.tile([P, S], F32, name=f"y{c}")
            for lo, hi in pieces:
                acc = psum.tile([P, hi - lo], F32, name=f"acc{c}{lo}")
                for a in range(PASSES):
                    wq, ws = weights[c, a]
                    nc.tensor.matmul_mx(
                        out=acc[:],
                        lhsT=wq.bitcast(FP8X4),
                        lhsT_scale=ws,
                        rhs=xq[a][:, lo:hi].bitcast(FP8X4),
                        rhs_scale=xs[a][:, lo:hi],
                        start=(a == 0),
                        stop=(a == PASSES - 1),
                    )
                nc.scalar.activation(y[:, lo:hi], acc[:], SILU, bias=bias[:, c : c + 1])
            ys.append(y)

        ys = []
        prepare_w(0, 1, False)
        results(0, PIECES)
        prepare_w(1, 1, True)
        results(1, [(0, S)])

        terms, sums, outs = {}, {}, {}
        for c0, count in ((0, 2), (2, 1), (3, 1)):
            terms[c0] = keep.tile([P, count, D, V], F32, name=f"terms{c0}")
            sums[c0] = keep.tile([P, count, V], F32, name=f"sums{c0}")
            outs[c0] = keep.tile([P, count, V], F32, name=f"outs{c0}")

        def fetch(c, d, c0):
            nc.vector.tensor_tensor(
                terms[c0][:, c - c0, d, :], ys[c][:].indirect(pos_sb[d][:]), gates[c][:, d, :], MULT
            )

        def add_first(c0):
            nc.vector.tensor_tensor(sums[c0][:], terms[c0][:, :, 0, :], terms[c0][:, :, 1, :], ADD)

        def add_last(c0, count):
            nc.vector.tensor_tensor(outs[c0][:], sums[c0][:], terms[c0][:, :, 2, :], ADD)
            rows = out[c0 * P : (c0 + count) * P, :]
            nc.sync.dma_start(rows.rearrange("(c p) v -> p c v", p=P), outs[c0][:])

        fetch(0, 0, 0)
        fetch(0, 1, 0)
        prepare_w(2, 2, True)
        results(2, [(0, S)])
        results(3, [(0, S)])
        fetch(0, 2, 0)
        for d in range(D):
            fetch(1, d, 0)
        fetch(2, 0, 2)
        add_first(0)
        fetch(2, 1, 2)
        add_last(0, 2)
        fetch(2, 2, 2)
        fetch(3, 0, 3)
        add_first(2)
        fetch(3, 1, 3)
        fetch(3, 2, 3)
        add_first(3)
        add_last(2, 1)
        add_last(3, 1)
